import numpy as np
import ml_dtypes


def mxq(x, axis, fmt="e4m3"):
    dtype, down = {"e4m3": (ml_dtypes.float8_e4m3fn, 7), "e5m2": (ml_dtypes.float8_e5m2, 14)}[fmt]
    v = np.moveaxis(np.asarray(x, np.float32).astype(ml_dtypes.bfloat16).astype(np.float64), axis, -1)
    blocks = v.reshape(v.shape[:-1] + (-1, 32))
    amax = np.abs(blocks).max(-1, keepdims=True)
    byte = np.maximum(np.where(amax > 0, np.frexp(amax)[1] - 1 + 127, 0) - down, 1)
    scale = np.exp2(byte - 127.0)
    codes = (blocks / scale).astype(np.float32).astype(dtype).astype(np.float64)
    return np.moveaxis((codes * scale).reshape(v.shape), -1, axis)


WIDE = False


def mx_kscale(k):
    if not WIDE:
        return np.ones(k)
    levels = np.array([18, -18])
    if k % 512:
        return np.exp2(np.random.permutation(np.resize(levels, k // 32))).repeat(32)
    a = np.empty((k // 512, 16))
    for p in range(k // 512):
        a[p, :8] = np.random.permutation(np.resize(levels, 8))
        for g in range(8):
            far = levels[np.abs(levels - a[p, g]) >= 10]
            a[p, g + 8] = far[np.random.randint(len(far))]
    return np.exp2(a.ravel()).repeat(32)


def f64(x):
    return np.asarray(x).astype(np.float64)


def striped(idx):
    return np.tile(np.asarray(idx).reshape(-1, 16).T, (8, 1)).astype(np.uint16)


def unstriped(offs):
    return offs[:16].T.reshape(-1).astype(np.int64)


E2M1 = np.array([0.0, 0.5, 1.0, 1.5, 2.0, 3.0, 4.0, 6.0, -0.0, -0.5, -1.0, -1.5, -2.0, -3.0, -4.0, -6.0])


def pack_weight(w, fmt):
    k, n = w.shape
    w = f64(np.asarray(w, np.float32).astype(ml_dtypes.bfloat16)).reshape(k // 32, 32, n)
    amax = np.abs(w).max(1)
    if fmt == "e4m3":
        byte = np.frexp(amax)[1] - 1 + 127 - 7
    else:
        mant, ex = np.frexp(amax / 6.0)
        byte = np.where(mant > 0.5, ex, ex - 1) + 127
    byte = np.clip(np.where(amax > 0, byte, 1), 1, 254)
    scaled = (w * np.exp2(127.0 - byte)[:, None, :]).reshape(k, n).astype(np.float32)
    by_word = np.ascontiguousarray(scaled.reshape(k // 512, 128, 4, n).transpose(0, 1, 3, 2))
    if fmt == "e4m3":
        words = by_word.astype(ml_dtypes.float8_e4m3fn).view(np.uint8)
    else:
        c = by_word.astype(ml_dtypes.float4_e2m1fn).view(np.uint8) & 0xF
        words = (c[..., 0::2] | (c[..., 1::2] << 4)).reshape(k // 512, 128, 2 * n)
    return np.ascontiguousarray(words), np.ascontiguousarray(byte.astype(np.uint8).reshape(k // 512, 16, n))


def unpack_weight(words, scales, fmt):
    g, _, n = scales.shape
    words = np.ascontiguousarray(words).reshape(g, 128, n, -1)
    if fmt == "e4m3":
        vals = words.view(ml_dtypes.float8_e4m3fn).astype(np.float64)
    else:
        nib = np.empty((g, 128, n, 4), np.uint8)
        nib[..., 0::2] = words & 0xF
        nib[..., 1::2] = words >> 4
        vals = E2M1[nib]
    vals = vals * np.repeat(np.exp2(scales.astype(np.float64) - 127.0), 8, axis=1)[..., None]
    return vals.transpose(0, 1, 3, 2).reshape(g * 512, n)


def planes(y):
    n, m = y.shape
    v = y.astype(np.float32).astype(ml_dtypes.bfloat16).astype(np.float64).reshape(n // 32, 32, m)
    top = np.abs(v).max(1)
    byte = np.clip(np.where(top > 0, np.frexp(top)[1] - 1 + 127 - 7, 1), 1, 254)
    codes = (v * np.exp2(127.0 - byte)[:, None, :]).reshape(n, m).astype(np.float32).astype(ml_dtypes.float8_e4m3fn).view(np.uint8)
    words = codes.reshape(n // 512, 128, 4, m).transpose(0, 1, 3, 2)
    return np.ascontiguousarray(words), np.ascontiguousarray(byte.astype(np.uint8).reshape(n // 512, 16, m))


def setup_inputs():
    n = np.random.standard_normal
    uni = np.random.uniform
    nbr = np.random.randint(0, 512, 1024)
    f_m = mx_kscale(512)
    W_ = pack_weight(n((512, 512)) / np.sqrt(512) * f_m[:, None], "e4m3")
    return {
        "W_words": W_[0],
        "W_scales": W_[1],
        "dyT": (n((512, 512)) / f_m[:, None]).astype(np.float32),
        "fil": (n((512, 1024))).astype(np.float32),
        "offs": striped(nbr),
    }


def reference(W_words, W_scales, dyT, fil, offs):
    nbr = unstriped(offs)
    W = unpack_weight(W_words, W_scales, "e4m3")
    u = W.T @ mxq(f64(dyT), 0, "e5m2")
    u_c = u[:, nbr]
    q = f64(fil) * u_c
    out_0 = q.reshape(512, 512, 2).sum(-1)
    return (out_0,) + planes(out_0)

@@ -1,0 +1,167 @@
+from contextlib import ExitStack
+
+import concourse.mybir as mybir
+
+F32 = mybir.dt.float32
+BF16 = mybir.dt.bfloat16
+I32 = mybir.dt.int32
+U32 = mybir.dt.uint32
+U16 = mybir.dt.uint16
+U8 = mybir.dt.uint8
+E4M3 = mybir.dt.float8_e4m3fn_x4
+E5M2 = mybir.dt.float8_e5m2_x4
+MULT = mybir.AluOpType.mult
+ADD = mybir.AluOpType.add
+
+P = 128
+PACK = 4
+D = 512
+X = 512
+DEG = 2
+FLOPS = 2 * 512 * D * X
+
+DY_CHUNKS = (256, 128, 128)
+X_CHUNKS = (128, 128, 128, 64, 64)
+
+
+def starts(widths):
+    return [(sum(widths[:i]), w) for i, w in enumerate(widths)]
+
+
+def tile_attend_gcfconv_x_pl_kernel(tc, W_words, W_scales, dyT, fil, offs, out_0, out_1, out_2):
+    nc = tc.nc
+    with ExitStack() as ctx:
+        keep = ctx.enter_context(tc.tile_pool(name="keep", bufs=1))
+        psum = ctx.enter_context(tc.psum_pool(name="psum", bufs=1))
+
+        offsets = keep.tile([P, X * DEG // 16], U16, name="offsets")
+        w_raw = keep.tile([P, D], I32, name="w_raw", align_bytes=64)
+        ws_raw = keep.tile([P, D], U8, name="ws_raw", align_bytes=64)
+        w_codes = keep.tile([P, D], I32, name="w_codes", align_bytes=64)
+        w_scales = keep.tile([P, D], U8, name="w_scales", align_bytes=64)
+
+        nc.vector.memset(ws_raw[:].bitcast(I32), 0)
+        for q in range(4):
+            nc.scalar.dma_start(
+                out=ws_raw[32 * q : 32 * q + 4, :].bitcast(I32),
+                in_=W_scales[0][4 * q : 4 * q + 4, :].bitcast(I32),
+            )
+
+        dy_rows = dyT.rearrange("(p j) x -> p j x", j=PACK)
+        dy_raw = []
+        for c, (x0, w) in enumerate(starts(DY_CHUNKS)):
+            raw = keep.tile([P, PACK, w], F32, name="dy_raw%d" % c)
+            nc.sync.dma_start(out=raw[:], in_=dy_rows[:, :, x0 : x0 + w])
+            dy_raw.append(raw)
+        nc.sync.dma_start(out=w_raw[:], in_=W_words[0].rearrange("p n t -> p (n t)").bitcast(I32))
+        nc.sync.dma_start(offsets[:], offs)
+
+        fil_rows = fil.rearrange("(p t) e -> p t e", t=PACK)
+        fil_sb = []
+        for c, (x0, w) in enumerate(starts(X_CHUNKS)):
+            f = keep.tile([P, PACK, DEG * w], F32, name="fil%d" % c)
+            nc.sync.dma_start(out=f[:], in_=fil_rows[:, :, DEG * x0 : DEG * (x0 + w)])
+            fil_sb.append(f)
+
+        nc.vector.tensor_copy(
+            out=w_scales[:].rearrange("p (t m) -> p t m", t=PACK),
+            in_=ws_raw[:].rearrange("p (m t) -> p t m", t=PACK),
+        )
+
+        dy_codes = keep.tile([P, X], U32, name="dy_codes", align_bytes=64)
+        dy_scales = keep.tile([P, X], U8, name="dy_scales", align_bytes=64)
+        dy_bf = []
+        for c, (x0, w) in enumerate(starts(DY_CHUNKS)):
+            g = keep.tile([P, w, PACK], BF16, name="dy_bf%d" % c, align_bytes=64)
+            dst = g[:].rearrange("p (c i) j -> p c j i", i=4)
+            src = dy_raw[c][:].rearrange("p j (c i) -> p c j i", i=4)
+            if c == 0:
+                nc.scalar.copy(out=dst, in_=src)
+            else:
+                nc.vector.tensor_copy(out=dst, in_=src)
+            dy_bf.append(g)
+        w_dealt = w_codes[:].rearrange("p (t m) -> p t m", t=PACK)
+        w_cols = w_raw[:].rearrange("p (m t) -> p t m", t=PACK)
+        for c, (x0, w) in enumerate(starts(DY_CHUNKS)):
+            if c == len(DY_CHUNKS) - 1:
+                nc.vector.tensor_copy(out=w_dealt[:, 0, :], in_=w_cols[:, 0, :])
+            nc.vector.quantize_mx(
+                out=dy_codes[:, x0 : x0 + w].bitcast(E5M2),
+                scales=dy_scales[:, x0 : x0 + w],
+                in_=dy_bf[c][:].rearrange("p w j -> p (w j)"),
+            )
+
+        nc.vector.tensor_copy(out=w_dealt[:, 1:, :], in_=w_cols[:, 1:, :])
+
+        u = []
+        for t in range(PACK):
+            acc = psum.tile([P, X], F32, name="acc%d" % t)
+            nc.tensor.matmul_mx(
+                out=acc[:],
+                lhsT=w_codes[:, P * t : P * (t + 1)].bitcast(E4M3),
+                lhsT_scale=w_scales[:, P * t : P * (t + 1)],
+                rhs=dy_codes[:].bitcast(E5M2),
+                rhs_scale=dy_scales[:],
+                start=True,
+                stop=True,
+            )
+            u_t = keep.tile([P, X], F32, name="u%d" % t)
+            nc.scalar.copy(out=u_t[:], in_=acc[:])
+            u.append(u_t)
+
+        out_rows = out_0.rearrange("(p t) x -> p t x", t=PACK)
+        words_out = out_1[0].rearrange("p x t -> p (x t)").bitcast(I32)
+        y_codes = keep.tile([P, X], U32, name="y_codes", align_bytes=64)
+        y_scales = keep.tile([P, X], U8, name="y_scales", align_bytes=64)
+        chunks = starts(X_CHUNKS)
+        last = len(chunks) - 1
+        q_sb = [keep.tile([P, PACK, DEG * w], F32, name="q%d" % c) for c, (x0, w) in enumerate(chunks)]
+        y_sb = [keep.tile([P, PACK, w], F32, name="y%d" % c) for c, (x0, w) in enumerate(chunks)]
+        y_bf = [keep.tile([P, w, PACK], BF16, name="y_bf%d" % c, align_bytes=64) for c, (x0, w) in enumerate(chunks)]
+
+        def gather(c, t):
+            x0, w = chunks[c]
+            cols = offsets[:, DEG * x0 // 16 : DEG * (x0 + w) // 16]
+            nc.vector.tensor_tensor(q_sb[c][:, t, :], u[t][:].indirect(cols), fil_sb[c][:, t, :], MULT)
+
+        def pair_sum(c):
+            x0, w = chunks[c]
+            pairs = q_sb[c][:].rearrange("p t (x j) -> p t x j", j=DEG)
+            nc.vector.tensor_tensor(y_sb[c][:], pairs[:, :, :, 0], pairs[:, :, :, 1], ADD)
+            nc.sync.dma_start(out=out_rows[:, :, x0 : x0 + w], in_=y_sb[c][:])
+
+        def round_interleave(c):
+            nc.scalar.copy(
+                out=y_bf[c][:].rearrange("p (c i) t -> p c t i", i=4),
+                in_=y_sb[c][:].rearrange("p t (c i) -> p c t i", i=4),
+            )
+
+        def quantize(c):
+            x0, w = chunks[c]
+            nc.vector.quantize_mx(
+                out=y_codes[:, x0 : x0 + w].bitcast(E4M3),
+                scales=y_scales[:, x0 : x0 + w],
+                in_=y_bf[c][:].rearrange("p x t -> p (x t)"),
+            )
+            nc.sync.dma_start(out=words_out[:, x0 : x0 + w], in_=y_codes[:, x0 : x0 + w].bitcast(I32))
+
+        for c in range(len(chunks)):
+            gather(c, 0)
+            if c > 0:
+                pair_sum(c - 1)
+                round_interleave(c - 1)
+            gather(c, 1)
+            gather(c, 2)
+            gather(c, 3)
+            if c > 0:
+                quantize(c - 1)
+        pairs = q_sb[last][:].rearrange("p t (x j) -> p x t j", j=DEG)
+        nc.vector.tensor_tensor(y_bf[last][:], pairs[:, :, :, 0], pairs[:, :, :, 1], ADD)
+        pair_sum(last)
+        quantize(last)
+        for q in range(4):
+            eng = nc.scalar if q % 2 == 0 else nc.sync
+            eng.dma_start(
+                out=out_2[0][4 * q : 4 * q + 4, :].bitcast(I32),
+                in_=y_scales[32 * q : 32 * q + 4, :].bitcast(I32),
+            )

@@ -1,6 +1,7 @@
 from contextlib import ExitStack
 
 import concourse.mybir as mybir
+from concourse.masks import make_identity
 
 F32 = mybir.dt.float32
 BF16 = mybir.dt.bfloat16
@@ -20,8 +21,10 @@ X = 512
 DEG = 2
 FLOPS = 2 * 512 * D * X
 
-DY_CHUNKS = (256, 128, 128)
-X_CHUNKS = (128, 128, 128, 64, 64)
+DY_CHUNKS = (128, 128, 128, 128)
+X_CHUNKS = (256, 128, 128)
+PE_UNITS = 6
+PAD = 32
 
 
 def starts(widths):
@@ -32,15 +35,21 @@ def tile_attend_gcfconv_x_pl_kernel(tc, W_words, W_scales, dyT, fil, offs, out_0
     nc = tc.nc
     with ExitStack() as ctx:
         keep = ctx.enter_context(tc.tile_pool(name="keep", bufs=1))
+        stage = ctx.enter_context(tc.tile_pool(name="stage", bufs=2))
+        turn = ctx.enter_context(tc.psum_pool(name="turn", bufs=2))
         psum = ctx.enter_context(tc.psum_pool(name="psum", bufs=1))
 
         offsets = keep.tile([P, X * DEG // 16], U16, name="offsets")
         w_raw = keep.tile([P, D], I32, name="w_raw", align_bytes=64)
         ws_raw = keep.tile([P, D], U8, name="ws_raw", align_bytes=64)
         w_codes = keep.tile([P, D], I32, name="w_codes", align_bytes=64)
-        w_scales = keep.tile([P, D], U8, name="w_scales", align_bytes=64)
 
         nc.vector.memset(ws_raw[:].bitcast(I32), 0)
+        ident = keep.tile([P, P], F32, name="ident")
+        make_identity(nc, ident[:])
+        u = [keep.tile([P, X + PAD], F32, name="u%d" % t) for t in range(PACK)]
+        for t in range(PACK):
+            nc.gpsimd.memset(u[t][:, X:], 0.0)
         for q in range(4):
             nc.scalar.dma_start(
                 out=ws_raw[32 * q : 32 * q + 4, :].bitcast(I32),
@@ -50,7 +59,7 @@ def tile_attend_gcfconv_x_pl_kernel(tc, W_words, W_scales, dyT, fil, offs, out_0
         dy_rows = dyT.rearrange("(p j) x -> p j x", j=PACK)
         dy_raw = []
         for c, (x0, w) in enumerate(starts(DY_CHUNKS)):
-            raw = keep.tile([P, PACK, w], F32, name="dy_raw%d" % c)
+            raw = keep.tile([P, PACK, w], F32, name="dy_raw%d" % c, align_bytes=64)
             nc.sync.dma_start(out=raw[:], in_=dy_rows[:, :, x0 : x0 + w])
             dy_raw.append(raw)
         nc.sync.dma_start(out=w_raw[:], in_=W_words[0].rearrange("p n t -> p (n t)").bitcast(I32))
@@ -63,10 +72,6 @@ def tile_attend_gcfconv_x_pl_kernel(tc, W_words, W_scales, dyT, fil, offs, out_0
             nc.sync.dma_start(out=f[:], in_=fil_rows[:, :, DEG * x0 : DEG * (x0 + w)])
             fil_sb.append(f)
 
-        nc.vector.tensor_copy(
-            out=w_scales[:].rearrange("p (t m) -> p t m", t=PACK),
-            in_=ws_raw[:].rearrange("p (m t) -> p t m", t=PACK),
-        )
 
         dy_codes = keep.tile([P, X], U32, name="dy_codes", align_bytes=64)
         dy_scales = keep.tile([P, X], U8, name="dy_scales", align_bytes=64)
@@ -75,39 +80,44 @@ def tile_attend_gcfconv_x_pl_kernel(tc, W_words, W_scales, dyT, fil, offs, out_0
             g = keep.tile([P, w, PACK], BF16, name="dy_bf%d" % c, align_bytes=64)
             dst = g[:].rearrange("p (c i) j -> p c j i", i=4)
             src = dy_raw[c][:].rearrange("p j (c i) -> p c j i", i=4)
-            if c == 0:
+            if c % 2 == 0:
                 nc.scalar.copy(out=dst, in_=src)
             else:
                 nc.vector.tensor_copy(out=dst, in_=src)
             dy_bf.append(g)
         w_dealt = w_codes[:].rearrange("p (t m) -> p t m", t=PACK)
+        ws_cols = ws_raw[:].rearrange("p (m t) -> p t m", t=PACK)
+        ws_first = keep.tile([P, P], U8, name="ws_first", align_bytes=64)
         w_cols = w_raw[:].rearrange("p (m t) -> p t m", t=PACK)
         for c, (x0, w) in enumerate(starts(DY_CHUNKS)):
             if c == len(DY_CHUNKS) - 1:
-                nc.vector.tensor_copy(out=w_dealt[:, 0, :], in_=w_cols[:, 0, :])
+                nc.vector.tensor_copy(out=ws_first[:], in_=ws_cols[:, 0, :])
             nc.vector.quantize_mx(
                 out=dy_codes[:, x0 : x0 + w].bitcast(E5M2),
                 scales=dy_scales[:, x0 : x0 + w],
                 in_=dy_bf[c][:].rearrange("p w j -> p (w j)"),
             )
 
-        nc.vector.tensor_copy(out=w_dealt[:, 1:, :], in_=w_cols[:, 1:, :])
+        nc.vector.tensor_copy(out=w_dealt[:, 0, :], in_=w_cols[:, 0, :])
+        ws_rest = keep.tile([P, PACK - 1, P], U8, name="ws_rest", tag="dy_raw%d" % (len(DY_CHUNKS) - 1), align_bytes=64)
+        w_scales = [ws_first[:]]
+        for t in range(1, PACK):
+            nc.vector.tensor_copy(out=w_dealt[:, t, :], in_=w_cols[:, t, :])
+            nc.vector.tensor_copy(out=ws_rest[:, t - 1, :], in_=ws_cols[:, t, :])
+            w_scales.append(ws_rest[:, t - 1, :])
 
-        u = []
         for t in range(PACK):
             acc = psum.tile([P, X], F32, name="acc%d" % t)
             nc.tensor.matmul_mx(
                 out=acc[:],
                 lhsT=w_codes[:, P * t : P * (t + 1)].bitcast(E4M3),
-                lhsT_scale=w_scales[:, P * t : P * (t + 1)],
+                lhsT_scale=w_scales[t],
                 rhs=dy_codes[:].bitcast(E5M2),
                 rhs_scale=dy_scales[:],
                 start=True,
                 stop=True,
             )
-            u_t = keep.tile([P, X], F32, name="u%d" % t)
-            nc.scalar.copy(out=u_t[:], in_=acc[:])
-            u.append(u_t)
+            nc.scalar.copy(out=u[t][:, :X], in_=acc[:])
 
         out_rows = out_0.rearrange("(p t) x -> p t x", t=PACK)
         words_out = out_1[0].rearrange("p x t -> p (x t)").bitcast(I32)
@@ -115,23 +125,52 @@ def tile_attend_gcfconv_x_pl_kernel(tc, W_words, W_scales, dyT, fil, offs, out_0
         y_scales = keep.tile([P, X], U8, name="y_scales", align_bytes=64)
         chunks = starts(X_CHUNKS)
         last = len(chunks) - 1
-        q_sb = [keep.tile([P, PACK, DEG * w], F32, name="q%d" % c) for c, (x0, w) in enumerate(chunks)]
-        y_sb = [keep.tile([P, PACK, w], F32, name="y%d" % c) for c, (x0, w) in enumerate(chunks)]
-        y_bf = [keep.tile([P, w, PACK], BF16, name="y_bf%d" % c, align_bytes=64) for c, (x0, w) in enumerate(chunks)]
+        q_first = keep.tile([P, PACK, DEG * X_CHUNKS[0]], F32, name="q_first")
+        q_sb = [q_first[:]]
+        for c in range(1, len(chunks)):
+            spent = fil_sb[c - 1][:].rearrange("p t e -> p (t e)")
+            n = PACK * DEG * X_CHUNKS[c]
+            q_sb.append(spent[:, spent.shape[1] - n :].rearrange("p (t e) -> p t e", t=PACK))
+        y_sb = [keep.tile([P, PACK, w], F32, name="y%d" % c) for c, (x0, w) in enumerate(chunks[:last])]
+        y_bf = [
+            keep.tile([P, w, PACK], BF16, name="y_bf%d" % c, align_bytes=64) for c, (x0, w) in enumerate(chunks[:last])
+        ]
 
         def gather(c, t):
             x0, w = chunks[c]
             cols = offsets[:, DEG * x0 // 16 : DEG * (x0 + w) // 16]
             nc.vector.tensor_tensor(q_sb[c][:, t, :], u[t][:].indirect(cols), fil_sb[c][:, t, :], MULT)
 
-        def pair_sum(c):
+        def pair_sum(c, t0):
+            pairs = q_sb[c][:, t0:, :].rearrange("p t (x j) -> p t x j", j=DEG)
+            nc.vector.tensor_tensor(y_sb[c][:, t0:, :], pairs[:, :, :, 0], pairs[:, :, :, 1], ADD)
+
+        def store(c):
             x0, w = chunks[c]
-            pairs = q_sb[c][:].rearrange("p t (x j) -> p t x j", j=DEG)
-            nc.vector.tensor_tensor(y_sb[c][:], pairs[:, :, :, 0], pairs[:, :, :, 1], ADD)
             nc.sync.dma_start(out=out_rows[:, :, x0 : x0 + w], in_=y_sb[c][:])
 
-        def round_interleave(c):
-            nc.scalar.copy(
+        def sum_turned(c, t):
+            blocks = chunks[c][1] // P
+            bank = turn.tile([P, blocks, P], F32, name="summed")
+            pairs = q_sb[c][:, t, :].rearrange("p (b x j) -> p b x j", x=P, j=DEG)
+            for b in range(blocks):
+                for j in range(DEG):
+                    nc.tensor.matmul(
+                        bank[:, b, :], pairs[:, b, :, j], ident[:], start=(j == 0), stop=(j == DEG - 1), is_transpose=True
+                    )
+            turned = stage.tile([P, blocks, P], F32, name="turned")
+            nc.scalar.copy(out=turned[:], in_=bank[:])
+            return turned
+
+        def turn_back(c, t, turned):
+            blocks = chunks[c][1] // P
+            bank = turn.tile([P, blocks, P], F32, name="back")
+            for b in range(blocks):
+                nc.tensor.transpose(bank[:, b, :], turned[:, b, :], ident[:])
+            nc.scalar.copy(out=y_sb[c][:, t, :], in_=bank[:].rearrange("p b x -> p (b x)"))
+
+        def round_interleave(c, copy):
+            copy(
                 out=y_bf[c][:].rearrange("p (c i) t -> p c t i", i=4),
                 in_=y_sb[c][:].rearrange("p t (c i) -> p c t i", i=4),
             )
@@ -145,19 +184,28 @@ def tile_attend_gcfconv_x_pl_kernel(tc, W_words, W_scales, dyT, fil, offs, out_0
             )
             nc.sync.dma_start(out=words_out[:, x0 : x0 + w], in_=y_codes[:, x0 : x0 + w].bitcast(I32))
 
+        pending = None
         for c in range(len(chunks)):
-            gather(c, 0)
-            if c > 0:
-                pair_sum(c - 1)
-                round_interleave(c - 1)
-            gather(c, 1)
-            gather(c, 2)
-            gather(c, 3)
+            for t in range(PACK):
+                gather(c, t)
+                unit = PACK * c + t
+                turned = sum_turned(c, t) if unit < PE_UNITS else None
+                if pending is not None:
+                    turn_back(*pending)
+                pending = (c, t, turned) if unit < PE_UNITS else None
+                if c > 0 and t == 0:
+                    on_pe = min(max(PE_UNITS - PACK * (c - 1), 0), PACK)
+                    if on_pe < PACK:
+                        pair_sum(c - 1, on_pe)
+                    store(c - 1)
+                    round_interleave(c - 1, nc.scalar.copy)
             if c > 0:
                 quantize(c - 1)
-        pairs = q_sb[last][:].rearrange("p t (x j) -> p x t j", j=DEG)
-        nc.vector.tensor_tensor(y_bf[last][:], pairs[:, :, :, 0], pairs[:, :, :, 1], ADD)
-        pair_sum(last)
+        y_sb.append(keep.tile([P, PACK, X_CHUNKS[last]], F32, name="y_last", tag="y_bf0", align_bytes=64))
+        pair_sum(last, 0)
+        store(last)
+        y_bf.append(keep.tile([P, X_CHUNKS[last], PACK], BF16, name="y_bf_last", tag="y_bf1", align_bytes=64))
+        round_interleave(last, nc.vector.tensor_copy)
         quantize(last)
         for q in range(4):
             eng = nc.scalar if q % 2 == 0 else nc.sync

@@ -16,19 +16,25 @@ ADD = mybir.AluOpType.add
 
 P = 128
 PACK = 4
+QUADRANTS = 4
+M = 512
 D = 512
 X = 512
 DEG = 2
-FLOPS = 2 * 512 * D * X
+FLOPS = 2 * M * D * X
 
 DY_CHUNKS = (128, 128, 128, 128)
 X_CHUNKS = (256, 128, 128)
-PE_UNITS = 6
+TENSOR_SUMS = 6
 PAD = 32
 
 
 def starts(widths):
     return [(sum(widths[:i]), w) for i, w in enumerate(widths)]
+
+
+def interleave(copy, out, in_):
+    copy(out=out.rearrange("p (c i) t -> p c t i", i=4), in_=in_.rearrange("p t (c i) -> p c t i", i=4))
 
 
 def tile_attend_gcfconv_x_pl_kernel(tc, W_words, W_scales, dyT, fil, offs, out_0, out_1, out_2):
@@ -41,6 +47,7 @@ def tile_attend_gcfconv_x_pl_kernel(tc, W_words, W_scales, dyT, fil, offs, out_0
 
         offsets = keep.tile([P, X * DEG // 16], U16, name="offsets")
         w_raw = keep.tile([P, D], I32, name="w_raw", align_bytes=64)
+        ws_rows = keep.tile([P, D // 4], I32, name="ws_rows")
         ws_raw = keep.tile([P, D], U8, name="ws_raw", align_bytes=64)
         w_codes = keep.tile([P, D], I32, name="w_codes", align_bytes=64)
 
@@ -50,11 +57,6 @@ def tile_attend_gcfconv_x_pl_kernel(tc, W_words, W_scales, dyT, fil, offs, out_0
         u = [keep.tile([P, X + PAD], F32, name="u%d" % t) for t in range(PACK)]
         for t in range(PACK):
             nc.gpsimd.memset(u[t][:, X:], 0.0)
-        for q in range(4):
-            nc.scalar.dma_start(
-                out=ws_raw[32 * q : 32 * q + 4, :].bitcast(I32),
-                in_=W_scales[0][4 * q : 4 * q + 4, :].bitcast(I32),
-            )
 
         dy_rows = dyT.rearrange("(p j) x -> p j x", j=PACK)
         dy_raw = []
@@ -62,44 +64,51 @@ def tile_attend_gcfconv_x_pl_kernel(tc, W_words, W_scales, dyT, fil, offs, out_0
             raw = keep.tile([P, PACK, w], F32, name="dy_raw%d" % c, align_bytes=64)
             nc.sync.dma_start(out=raw[:], in_=dy_rows[:, :, x0 : x0 + w])
             dy_raw.append(raw)
+            if c == 0:
+                for q in range(QUADRANTS):
+                    nc.sync.dma_start(
+                        out=ws_rows[32 * q : 32 * q + 4, :],
+                        in_=W_scales[0][4 * q : 4 * q + 4, :].bitcast(I32),
+                    )
         nc.sync.dma_start(out=w_raw[:], in_=W_words[0].rearrange("p n t -> p (n t)").bitcast(I32))
         nc.sync.dma_start(offsets[:], offs)
 
+        chunks = starts(X_CHUNKS)
+        last = len(chunks) - 1
         fil_rows = fil.rearrange("(p t) e -> p t e", t=PACK)
         fil_sb = []
-        for c, (x0, w) in enumerate(starts(X_CHUNKS)):
+        for c, (x0, w) in enumerate(chunks):
             f = keep.tile([P, PACK, DEG * w], F32, name="fil%d" % c)
-            nc.sync.dma_start(out=f[:], in_=fil_rows[:, :, DEG * x0 : DEG * (x0 + w)])
+            for planes in (slice(0, 1), slice(1, PACK)) if c == 0 else (slice(0, PACK),):
+                nc.sync.dma_start(out=f[:, planes, :], in_=fil_rows[:, planes, DEG * x0 : DEG * (x0 + w)])
             fil_sb.append(f)
-
 
         dy_codes = keep.tile([P, X], U32, name="dy_codes", align_bytes=64)
         dy_scales = keep.tile([P, X], U8, name="dy_scales", align_bytes=64)
+        for q in range(QUADRANTS):
+            nc.vector.tensor_copy(out=ws_raw[32 * q : 32 * q + 4, :].bitcast(I32), in_=ws_rows[32 * q : 32 * q + 4, :])
+
+        last_dy = len(DY_CHUNKS) - 1
         dy_bf = []
-        for c, (x0, w) in enumerate(starts(DY_CHUNKS)):
-            g = keep.tile([P, w, PACK], BF16, name="dy_bf%d" % c, align_bytes=64)
-            dst = g[:].rearrange("p (c i) j -> p c j i", i=4)
-            src = dy_raw[c][:].rearrange("p j (c i) -> p c j i", i=4)
-            if c % 2 == 0:
-                nc.scalar.copy(out=dst, in_=src)
-            else:
-                nc.vector.tensor_copy(out=dst, in_=src)
-            dy_bf.append(g)
-        w_dealt = w_codes[:].rearrange("p (t m) -> p t m", t=PACK)
-        ws_cols = ws_raw[:].rearrange("p (m t) -> p t m", t=PACK)
+        for c, w in enumerate(DY_CHUNKS):
+            rounded = keep.tile([P, w, PACK], BF16, name="dy_bf%d" % c, align_bytes=64)
+            interleave(nc.scalar.copy if c < last_dy else nc.vector.tensor_copy, rounded[:], dy_raw[c][:])
+            dy_bf.append(rounded)
+
+        w_dealt = w_codes[:].rearrange("p (t i) -> p t i", t=PACK)
+        ws_cols = ws_raw[:].rearrange("p (i t) -> p t i", t=PACK)
         ws_first = keep.tile([P, P], U8, name="ws_first", align_bytes=64)
-        w_cols = w_raw[:].rearrange("p (m t) -> p t m", t=PACK)
+        w_cols = w_raw[:].rearrange("p (i t) -> p t i", t=PACK)
         for c, (x0, w) in enumerate(starts(DY_CHUNKS)):
-            if c == len(DY_CHUNKS) - 1:
+            if c == last_dy:
                 nc.vector.tensor_copy(out=ws_first[:], in_=ws_cols[:, 0, :])
             nc.vector.quantize_mx(
                 out=dy_codes[:, x0 : x0 + w].bitcast(E5M2),
                 scales=dy_scales[:, x0 : x0 + w],
                 in_=dy_bf[c][:].rearrange("p w j -> p (w j)"),
             )
-
         nc.vector.tensor_copy(out=w_dealt[:, 0, :], in_=w_cols[:, 0, :])
-        ws_rest = keep.tile([P, PACK - 1, P], U8, name="ws_rest", tag="dy_raw%d" % (len(DY_CHUNKS) - 1), align_bytes=64)
+        ws_rest = keep.tile([P, PACK - 1, P], U8, name="ws_rest", tag="dy_raw%d" % last_dy, align_bytes=64)
         w_scales = [ws_first[:]]
         for t in range(1, PACK):
             nc.vector.tensor_copy(out=w_dealt[:, t, :], in_=w_cols[:, t, :])
@@ -123,25 +132,22 @@ def tile_attend_gcfconv_x_pl_kernel(tc, W_words, W_scales, dyT, fil, offs, out_0
         words_out = out_1[0].rearrange("p x t -> p (x t)").bitcast(I32)
         y_codes = keep.tile([P, X], U32, name="y_codes", align_bytes=64)
         y_scales = keep.tile([P, X], U8, name="y_scales", align_bytes=64)
-        chunks = starts(X_CHUNKS)
-        last = len(chunks) - 1
+
         q_first = keep.tile([P, PACK, DEG * X_CHUNKS[0]], F32, name="q_first")
         q_sb = [q_first[:]]
         for c in range(1, len(chunks)):
             spent = fil_sb[c - 1][:].rearrange("p t e -> p (t e)")
             n = PACK * DEG * X_CHUNKS[c]
             q_sb.append(spent[:, spent.shape[1] - n :].rearrange("p (t e) -> p t e", t=PACK))
-        y_sb = [keep.tile([P, PACK, w], F32, name="y%d" % c) for c, (x0, w) in enumerate(chunks[:last])]
-        y_bf = [
-            keep.tile([P, w, PACK], BF16, name="y_bf%d" % c, align_bytes=64) for c, (x0, w) in enumerate(chunks[:last])
-        ]
+        y_sb = [keep.tile([P, PACK, w], F32, name="y%d" % c) for c, w in enumerate(X_CHUNKS[:last])]
+        y_bf = [keep.tile([P, w, PACK], BF16, name="y_bf%d" % c, align_bytes=64) for c, w in enumerate(X_CHUNKS[:last])]
 
         def gather(c, t):
             x0, w = chunks[c]
             cols = offsets[:, DEG * x0 // 16 : DEG * (x0 + w) // 16]
             nc.vector.tensor_tensor(q_sb[c][:, t, :], u[t][:].indirect(cols), fil_sb[c][:, t, :], MULT)
 
-        def pair_sum(c, t0):
+        def sum_on_vector(c, t0):
             pairs = q_sb[c][:, t0:, :].rearrange("p t (x j) -> p t x j", j=DEG)
             nc.vector.tensor_tensor(y_sb[c][:, t0:, :], pairs[:, :, :, 0], pairs[:, :, :, 1], ADD)
 
@@ -150,7 +156,7 @@ def tile_attend_gcfconv_x_pl_kernel(tc, W_words, W_scales, dyT, fil, offs, out_0
             nc.sync.dma_start(out=out_rows[:, :, x0 : x0 + w], in_=y_sb[c][:])
 
         def sum_turned(c, t):
-            blocks = chunks[c][1] // P
+            blocks = X_CHUNKS[c] // P
             bank = turn.tile([P, blocks, P], F32, name="summed")
             pairs = q_sb[c][:, t, :].rearrange("p (b x j) -> p b x j", x=P, j=DEG)
             for b in range(blocks):
@@ -163,17 +169,11 @@ def tile_attend_gcfconv_x_pl_kernel(tc, W_words, W_scales, dyT, fil, offs, out_0
             return turned
 
         def turn_back(c, t, turned):
-            blocks = chunks[c][1] // P
+            blocks = X_CHUNKS[c] // P
             bank = turn.tile([P, blocks, P], F32, name="back")
             for b in range(blocks):
                 nc.tensor.transpose(bank[:, b, :], turned[:, b, :], ident[:])
             nc.scalar.copy(out=y_sb[c][:, t, :], in_=bank[:].rearrange("p b x -> p (b x)"))
-
-        def round_interleave(c, copy):
-            copy(
-                out=y_bf[c][:].rearrange("p (c i) t -> p c t i", i=4),
-                in_=y_sb[c][:].rearrange("p t (c i) -> p c t i", i=4),
-            )
 
         def quantize(c):
             x0, w = chunks[c]
@@ -188,28 +188,30 @@ def tile_attend_gcfconv_x_pl_kernel(tc, W_words, W_scales, dyT, fil, offs, out_0
         for c in range(len(chunks)):
             for t in range(PACK):
                 gather(c, t)
-                unit = PACK * c + t
-                turned = sum_turned(c, t) if unit < PE_UNITS else None
+                on_tensor = PACK * c + t < TENSOR_SUMS
+                turned = sum_turned(c, t) if on_tensor else None
                 if pending is not None:
                     turn_back(*pending)
-                pending = (c, t, turned) if unit < PE_UNITS else None
+                pending = (c, t, turned) if on_tensor else None
                 if c > 0 and t == 0:
-                    on_pe = min(max(PE_UNITS - PACK * (c - 1), 0), PACK)
-                    if on_pe < PACK:
-                        pair_sum(c - 1, on_pe)
+                    planes_summed = min(TENSOR_SUMS - PACK * (c - 1), PACK)
+                    if planes_summed < PACK:
+                        sum_on_vector(c - 1, planes_summed)
                     store(c - 1)
-                    round_interleave(c - 1, nc.scalar.copy)
+                    interleave(nc.scalar.copy, y_bf[c - 1][:], y_sb[c - 1][:])
             if c > 0:
                 quantize(c - 1)
+
         y_sb.append(keep.tile([P, PACK, X_CHUNKS[last]], F32, name="y_last", tag="y_bf0", align_bytes=64))
-        pair_sum(last, 0)
+        sum_on_vector(last, 0)
         store(last)
         y_bf.append(keep.tile([P, X_CHUNKS[last], PACK], BF16, name="y_bf_last", tag="y_bf1", align_bytes=64))
-        round_interleave(last, nc.vector.tensor_copy)
+        interleave(nc.vector.tensor_copy, y_bf[last][:], y_sb[last][:])
         quantize(last)
-        for q in range(4):
-            eng = nc.scalar if q % 2 == 0 else nc.sync
-            eng.dma_start(
+
+        for q in range(QUADRANTS):
+            queue = nc.scalar if q % 2 == 0 else nc.sync
+            queue.dma_start(
                 out=out_2[0][4 * q : 4 * q + 4, :].bitcast(I32),
                 in_=y_scales[32 * q : 32 * q + 4, :].bitcast(I32),
             )

from contextlib import ExitStack

import concourse.mybir as mybir
from concourse.masks import make_identity

F32 = mybir.dt.float32
BF16 = mybir.dt.bfloat16
I32 = mybir.dt.int32
U32 = mybir.dt.uint32
U16 = mybir.dt.uint16
U8 = mybir.dt.uint8
E4M3 = mybir.dt.float8_e4m3fn_x4
E5M2 = mybir.dt.float8_e5m2_x4
MULT = mybir.AluOpType.mult
ADD = mybir.AluOpType.add

P = 128
PACK = 4
QUADRANTS = 4
M = 512
D = 512
X = 512
DEG = 2
FLOPS = 2 * M * D * X

DY_CHUNKS = (128, 128, 128, 128)
X_CHUNKS = (256, 128, 128)
TENSOR_SUMS = 6
PAD = 32


def starts(widths):
    return [(sum(widths[:i]), w) for i, w in enumerate(widths)]


def interleave(copy, out, in_):
    copy(out=out.rearrange("p (c i) t -> p c t i", i=4), in_=in_.rearrange("p t (c i) -> p c t i", i=4))


def tile_attend_gcfconv_x_pl_kernel(tc, W_words, W_scales, dyT, fil, offs, out_0, out_1, out_2):
    nc = tc.nc
    with ExitStack() as ctx:
        keep = ctx.enter_context(tc.tile_pool(name="keep", bufs=1))
        stage = ctx.enter_context(tc.tile_pool(name="stage", bufs=2))
        turn = ctx.enter_context(tc.psum_pool(name="turn", bufs=2))
        psum = ctx.enter_context(tc.psum_pool(name="psum", bufs=1))

        offsets = keep.tile([P, X * DEG // 16], U16, name="offsets")
        w_raw = keep.tile([P, D], I32, name="w_raw", align_bytes=64)
        ws_rows = keep.tile([P, D // 4], I32, name="ws_rows")
        ws_raw = keep.tile([P, D], U8, name="ws_raw", align_bytes=64)
        w_codes = keep.tile([P, D], I32, name="w_codes", align_bytes=64)

        nc.vector.memset(ws_raw[:].bitcast(I32), 0)
        ident = keep.tile([P, P], F32, name="ident")
        make_identity(nc, ident[:])
        u = [keep.tile([P, X + PAD], F32, name="u%d" % t) for t in range(PACK)]
        for t in range(PACK):
            nc.gpsimd.memset(u[t][:, X:], 0.0)

        dy_rows = dyT.rearrange("(p j) x -> p j x", j=PACK)
        dy_raw = []
        for c, (x0, w) in enumerate(starts(DY_CHUNKS)):
            raw = keep.tile([P, PACK, w], F32, name="dy_raw%d" % c, align_bytes=64)
            nc.sync.dma_start(out=raw[:], in_=dy_rows[:, :, x0 : x0 + w])
            dy_raw.append(raw)
            if c == 0:
                for q in range(QUADRANTS):
                    nc.sync.dma_start(
                        out=ws_rows[32 * q : 32 * q + 4, :],
                        in_=W_scales[0][4 * q : 4 * q + 4, :].bitcast(I32),
                    )
        nc.sync.dma_start(out=w_raw[:], in_=W_words[0].rearrange("p n t -> p (n t)").bitcast(I32))
        nc.sync.dma_start(offsets[:], offs)

        chunks = starts(X_CHUNKS)
        last = len(chunks) - 1
        fil_rows = fil.rearrange("(p t) e -> p t e", t=PACK)
        fil_sb = []
        for c, (x0, w) in enumerate(chunks):
            f = keep.tile([P, PACK, DEG * w], F32, name="fil%d" % c)
            for planes in (slice(0, 1), slice(1, PACK)) if c == 0 else (slice(0, PACK),):
                nc.sync.dma_start(out=f[:, planes, :], in_=fil_rows[:, planes, DEG * x0 : DEG * (x0 + w)])
            fil_sb.append(f)

        dy_codes = keep.tile([P, X], U32, name="dy_codes", align_bytes=64)
        dy_scales = keep.tile([P, X], U8, name="dy_scales", align_bytes=64)
        for q in range(QUADRANTS):
            nc.vector.tensor_copy(out=ws_raw[32 * q : 32 * q + 4, :].bitcast(I32), in_=ws_rows[32 * q : 32 * q + 4, :])

        last_dy = len(DY_CHUNKS) - 1
        dy_bf = []
        for c, w in enumerate(DY_CHUNKS):
            rounded = keep.tile([P, w, PACK], BF16, name="dy_bf%d" % c, align_bytes=64)
            interleave(nc.scalar.copy if c < last_dy else nc.vector.tensor_copy, rounded[:], dy_raw[c][:])
            dy_bf.append(rounded)

        w_dealt = w_codes[:].rearrange("p (t i) -> p t i", t=PACK)
        ws_cols = ws_raw[:].rearrange("p (i t) -> p t i", t=PACK)
        ws_first = keep.tile([P, P], U8, name="ws_first", align_bytes=64)
        w_cols = w_raw[:].rearrange("p (i t) -> p t i", t=PACK)
        for c, (x0, w) in enumerate(starts(DY_CHUNKS)):
            if c == last_dy:
                nc.vector.tensor_copy(out=ws_first[:], in_=ws_cols[:, 0, :])
            nc.vector.quantize_mx(
                out=dy_codes[:, x0 : x0 + w].bitcast(E5M2),
                scales=dy_scales[:, x0 : x0 + w],
                in_=dy_bf[c][:].rearrange("p w j -> p (w j)"),
            )
        nc.vector.tensor_copy(out=w_dealt[:, 0, :], in_=w_cols[:, 0, :])
        ws_rest = keep.tile([P, PACK - 1, P], U8, name="ws_rest", tag="dy_raw%d" % last_dy, align_bytes=64)
        w_scales = [ws_first[:]]
        for t in range(1, PACK):
            nc.vector.tensor_copy(out=w_dealt[:, t, :], in_=w_cols[:, t, :])
            nc.vector.tensor_copy(out=ws_rest[:, t - 1, :], in_=ws_cols[:, t, :])
            w_scales.append(ws_rest[:, t - 1, :])

        for t in range(PACK):
            acc = psum.tile([P, X], F32, name="acc%d" % t)
            nc.tensor.matmul_mx(
                out=acc[:],
                lhsT=w_codes[:, P * t : P * (t + 1)].bitcast(E4M3),
                lhsT_scale=w_scales[t],
                rhs=dy_codes[:].bitcast(E5M2),
                rhs_scale=dy_scales[:],
                start=True,
                stop=True,
            )
            nc.scalar.copy(out=u[t][:, :X], in_=acc[:])

        out_rows = out_0.rearrange("(p t) x -> p t x", t=PACK)
        words_out = out_1[0].rearrange("p x t -> p (x t)").bitcast(I32)
        y_codes = keep.tile([P, X], U32, name="y_codes", align_bytes=64)
        y_scales = keep.tile([P, X], U8, name="y_scales", align_bytes=64)

        q_first = keep.tile([P, PACK, DEG * X_CHUNKS[0]], F32, name="q_first")
        q_sb = [q_first[:]]
        for c in range(1, len(chunks)):
            spent = fil_sb[c - 1][:].rearrange("p t e -> p (t e)")
            n = PACK * DEG * X_CHUNKS[c]
            q_sb.append(spent[:, spent.shape[1] - n :].rearrange("p (t e) -> p t e", t=PACK))
        y_sb = [keep.tile([P, PACK, w], F32, name="y%d" % c) for c, w in enumerate(X_CHUNKS[:last])]
        y_bf = [keep.tile([P, w, PACK], BF16, name="y_bf%d" % c, align_bytes=64) for c, w in enumerate(X_CHUNKS[:last])]

        def gather(c, t):
            x0, w = chunks[c]
            cols = offsets[:, DEG * x0 // 16 : DEG * (x0 + w) // 16]
            nc.vector.tensor_tensor(q_sb[c][:, t, :], u[t][:].indirect(cols), fil_sb[c][:, t, :], MULT)

        def sum_on_vector(c, t0):
            pairs = q_sb[c][:, t0:, :].rearrange("p t (x j) -> p t x j", j=DEG)
            nc.vector.tensor_tensor(y_sb[c][:, t0:, :], pairs[:, :, :, 0], pairs[:, :, :, 1], ADD)

        def store(c):
            x0, w = chunks[c]
            nc.sync.dma_start(out=out_rows[:, :, x0 : x0 + w], in_=y_sb[c][:])

        def sum_turned(c, t):
            blocks = X_CHUNKS[c] // P
            bank = turn.tile([P, blocks, P], F32, name="summed")
            pairs = q_sb[c][:, t, :].rearrange("p (b x j) -> p b x j", x=P, j=DEG)
            for b in range(blocks):
                for j in range(DEG):
                    nc.tensor.matmul(
                        bank[:, b, :], pairs[:, b, :, j], ident[:], start=(j == 0), stop=(j == DEG - 1), is_transpose=True
                    )
            turned = stage.tile([P, blocks, P], F32, name="turned")
            nc.scalar.copy(out=turned[:], in_=bank[:])
            return turned

        def turn_back(c, t, turned):
            blocks = X_CHUNKS[c] // P
            bank = turn.tile([P, blocks, P], F32, name="back")
            for b in range(blocks):
                nc.tensor.transpose(bank[:, b, :], turned[:, b, :], ident[:])
            nc.scalar.copy(out=y_sb[c][:, t, :], in_=bank[:].rearrange("p b x -> p (b x)"))

        def quantize(c):
            x0, w = chunks[c]
            nc.vector.quantize_mx(
                out=y_codes[:, x0 : x0 + w].bitcast(E4M3),
                scales=y_scales[:, x0 : x0 + w],
                in_=y_bf[c][:].rearrange("p x t -> p (x t)"),
            )
            nc.sync.dma_start(out=words_out[:, x0 : x0 + w], in_=y_codes[:, x0 : x0 + w].bitcast(I32))

        pending = None
        for c in range(len(chunks)):
            for t in range(PACK):
                gather(c, t)
                on_tensor = PACK * c + t < TENSOR_SUMS
                turned = sum_turned(c, t) if on_tensor else None
                if pending is not None:
                    turn_back(*pending)
                pending = (c, t, turned) if on_tensor else None
                if c > 0 and t == 0:
                    planes_summed = min(TENSOR_SUMS - PACK * (c - 1), PACK)
                    if planes_summed < PACK:
                        sum_on_vector(c - 1, planes_summed)
                    store(c - 1)
                    interleave(nc.scalar.copy, y_bf[c - 1][:], y_sb[c - 1][:])
            if c > 0:
                quantize(c - 1)

        y_sb.append(keep.tile([P, PACK, X_CHUNKS[last]], F32, name="y_last", tag="y_bf0", align_bytes=64))
        sum_on_vector(last, 0)
        store(last)
        y_bf.append(keep.tile([P, X_CHUNKS[last], PACK], BF16, name="y_bf_last", tag="y_bf1", align_bytes=64))
        interleave(nc.vector.tensor_copy, y_bf[last][:], y_sb[last][:])
        quantize(last)

        for q in range(QUADRANTS):
            queue = nc.scalar if q % 2 == 0 else nc.sync
            queue.dma_start(
                out=out_2[0][4 * q : 4 * q + 4, :].bitcast(I32),
                in_=y_scales[32 * q : 32 * q + 4, :].bitcast(I32),
            )
